import numpy as np
import ml_dtypes


def mxq(x, axis, fmt="e4m3"):
    dtype, down = {"e4m3": (ml_dtypes.float8_e4m3fn, 7), "e5m2": (ml_dtypes.float8_e5m2, 14)}[fmt]
    v = np.moveaxis(np.asarray(x, np.float32).astype(ml_dtypes.bfloat16).astype(np.float64), axis, -1)
    blocks = v.reshape(v.shape[:-1] + (-1, 32))
    amax = np.abs(blocks).max(-1, keepdims=True)
    byte = np.maximum(np.where(amax > 0, np.frexp(amax)[1] - 1 + 127, 0) - down, 1)
    scale = np.exp2(byte - 127.0)
    codes = (blocks / scale).astype(np.float32).astype(dtype).astype(np.float64)
    return np.moveaxis((codes * scale).reshape(v.shape), -1, axis)


WIDE = False


def mx_kscale(k):
    if not WIDE:
        return np.ones(k)
    levels = np.array([10, -10, 5, -5, 0])
    if k % 512:
        return np.exp2(np.random.permutation(np.resize(levels, k // 32))).repeat(32)
    a = np.empty((k // 512, 16))
    for p in range(k // 512):
        a[p, :8] = np.random.permutation(np.resize(levels, 8))
        for g in range(8):
            far = levels[np.abs(levels - a[p, g]) >= 10]
            a[p, g + 8] = far[np.random.randint(len(far))]
    return np.exp2(a.ravel()).repeat(32)


def f64(x):
    return np.asarray(x).astype(np.float64)


def striped(idx):
    return np.tile(idx.reshape(-1, 16).T, (8, 1)).astype(np.uint16)


def unstriped(offs):
    return offs[:16].T.reshape(-1).astype(np.int64)


def striped8(idx):
    return np.concatenate([x.reshape(-1, 16).T for x in idx]).astype(np.uint16)


def runs(offs, k):
    lists = np.stack([offs[16 * r : 16 * r + 16].T.reshape(-1) for r in range(8)]).astype(np.int64)
    return lists[np.arange(k) % 512 // 64]


def pack_weight(w):
    k, n = w.shape
    w = f64(np.asarray(w, np.float32).astype(ml_dtypes.bfloat16)).reshape(k // 32, 32, n)
    amax = np.abs(w).max(1)
    byte = np.clip(np.where(amax > 0, np.frexp(amax)[1] - 1 + 127 - 7, 1), 1, 254)
    scaled = (w * np.exp2(127.0 - byte)[:, None, :]).reshape(k, n).astype(np.float32)
    words = np.ascontiguousarray(scaled.reshape(k // 512, 128, 4, n).transpose(0, 1, 3, 2)).astype(ml_dtypes.float8_e4m3fn).view(np.uint8)
    return words, np.ascontiguousarray(byte.astype(np.uint8).reshape(k // 512, 16, n))


def unpack_weight(words, scales):
    g, p, n, _ = words.shape
    vals = np.ascontiguousarray(words).view(ml_dtypes.float8_e4m3fn).astype(np.float64) * np.repeat(np.exp2(scales.astype(np.float64) - 127.0), 8, axis=1)[..., None]
    return vals.transpose(0, 1, 3, 2).reshape(g * 512, n)


def sigmoid(v):
    return 1.0 / (1.0 + np.exp(-np.maximum(v, -700.0)))

def planes(y):
    n, m = y.shape
    v = y.astype(np.float32).astype(ml_dtypes.bfloat16).astype(np.float64).reshape(n // 32, 32, m)
    top = np.abs(v).max(1)
    byte = np.clip(np.where(top > 0, np.frexp(top)[1] - 1 + 127 - 7, 1), 1, 254)
    codes = (v * np.exp2(127.0 - byte)[:, None, :]).reshape(n, m).astype(np.float32).astype(ml_dtypes.float8_e4m3fn).view(np.uint8)
    words = codes.reshape(n // 512, 128, 4, m).transpose(0, 1, 3, 2)
    return np.ascontiguousarray(words), np.ascontiguousarray(byte.astype(np.uint8).reshape(n // 512, 16, m))


K, T, S, N, H, W = 512, 2048, 256, 512, 512, 1024


def setup_inputs():
    n = np.random.standard_normal
    s = mx_kscale(K)[:, None]
    u = mx_kscale(H)
    packed_xT = pack_weight(n((K, T)) * s)
    packed_w1 = pack_weight(n((K, H)) / np.sqrt(K) / s)
    packed_w2 = pack_weight(n((K, H)) / np.sqrt(K) / s)
    packed_w3 = pack_weight(n((H, N)) / np.sqrt(2 * H) / u[:, None])
    packed_w4 = pack_weight(n((H, N)) / np.sqrt(2 * H) / u[:, None])
    return {
        "x_words": packed_xT[0],
        "x_scales": packed_xT[1],
        "w1_words": packed_w1[0],
        "w1_scales": packed_w1[1],
        "w2_words": packed_w2[0],
        "w2_scales": packed_w2[1],
        "sl": np.random.uniform(1.0, 2.0, (H, 1)).astype(np.float32),
        "gn": (np.random.uniform(0.5, 1.5, (H, 1)) * u[:, None]).astype(np.float32),
        "gm": (np.random.uniform(0.5, 1.5, (H, 1)) * u[:, None]).astype(np.float32),
        "w3_words": packed_w3[0],
        "w3_scales": packed_w3[1],
        "w4_words": packed_w4[0],
        "w4_scales": packed_w4[1],
        "tau": np.random.uniform(0.3, 0.9, (N, 1)).astype(np.float32),
        "offs": striped(np.random.permutation(T)[:S]),
        "hz": striped8(np.random.randint(0, T, (8, S))),
        "n1": striped8(np.stack([np.random.permutation(S) for _ in range(8)])),
        "n2": striped8(np.stack([np.random.permutation(S) for _ in range(8)])),
        "n3": striped8(np.stack([np.random.permutation(S) for _ in range(8)])),
        "n4": striped8(np.stack([np.random.permutation(S) for _ in range(8)])),
        "n5": striped(np.random.randint(0, S, W)),
    }


def reference(x_words, x_scales, w1_words, w1_scales, w2_words, w2_scales, sl, gn, gm, w3_words, w3_scales, w4_words, w4_scales, tau, offs, hz, n1, n2, n3, n4, n5):
    xq = unpack_weight(x_words, x_scales)[:, unstriped(offs)]
    y = unpack_weight(w1_words, w1_scales).T @ xq
    mu = y.mean(axis=1, keepdims=True)
    sg = sigmoid(f64(sl) * (y[np.arange(H)[:, None], runs(n1, H)] - mu))
    z = f64(gn) * ((y - mu) * sg)
    x_hz = unpack_weight(x_words, x_scales)[np.arange(K)[:, None], runs(hz, K)]
    d = unpack_weight(w2_words, w2_scales).T @ x_hz
    z2 = f64(gm) * (0.75 * (d * (d[np.arange(H)[:, None], runs(n2, H)]) + (d[np.arange(H)[:, None], runs(n3, H)]) * (d[np.arange(H)[:, None], runs(n4, H)])))
    h = unpack_weight(w3_words, w3_scales).T @ mxq(z, 0, "e4m3") + unpack_weight(w4_words, w4_scales).T @ mxq(z2, 0, "e4m3")
    top = h.max(axis=1, keepdims=True)
    ea = np.exp(f64(tau) * (h[:, unstriped(n5)] - top))
    mx = ea.reshape(N, S, 4).max(axis=2)
    mn = ea.reshape(N, S, 4).min(axis=2)
    out_0 = 3.0 * (h * (mx - mn))
    return (out_0,) + planes(out_0)

@@ -1,0 +1,262 @@
+from contextlib import ExitStack
+
+import concourse.mybir as mybir
+
+F32 = mybir.dt.float32
+BF16 = mybir.dt.bfloat16
+I32 = mybir.dt.int32
+U32 = mybir.dt.uint32
+U16 = mybir.dt.uint16
+U8 = mybir.dt.uint8
+FP8X4 = mybir.dt.float8_e4m3fn_x4
+ALU = mybir.AluOpType
+ACT = mybir.ActivationFunctionType
+
+P = 128
+T = 2048
+S = 256
+C = 512
+R = 4
+HALF = 128
+WIN = 512
+FLOPS = 4 * 2 * 512 * 512 * 256
+
+
+def tile_picked_hjoinecndotegp_none_po_kernel(
+    tc, x_words, x_scales, w1_words, w1_scales, w2_words, w2_scales, sl, gn, gm,
+    w3_words, w3_scales, w4_words, w4_scales, tau, offs, hz, n1, n2, n3, n4, n5,
+    out_0, out_1, out_2,
+):
+    nc = tc.nc
+    with ExitStack() as ctx:
+        keep = ctx.enter_context(tc.tile_pool(name="keep", bufs=1))
+        psum = ctx.enter_context(tc.psum_pool(name="psum", bufs=1))
+
+        def tile(name, shape, dtype):
+            return keep.tile(shape, dtype, name=name, align_bytes=64)
+
+        def load_list(name, src):
+            t = keep.tile([P, src.shape[1]], U16, name=name)
+            nc.sync.dma_start(t[:], src)
+            return t
+
+        def load_words(name, src, width):
+            t = tile(name, [P, width], U32)
+            nc.sync.dma_start(t[:].bitcast(I32), src[0].rearrange("p n t -> p (n t)").bitcast(I32))
+            return t
+
+        def load_scale_rows(queue, plane, first, src):
+            for q in range(4):
+                queue.dma_start(plane[32 * q + first : 32 * q + first + 4, :].bitcast(I32), src[0, 4 * q : 4 * q + 4, :].bitcast(I32))
+
+        def load_vec(queue, name, src):
+            t = tile(name, [P, R], F32)
+            queue.dma_start(t[:], src.rearrange("(p t) o -> p (t o)", t=R))
+            return t
+
+        def deal(copy, name, src, dtype):
+            t = tile(name, [P, C], dtype)
+            copy(t[:].rearrange("p (t m) -> p t m", t=R), src[:].rearrange("p (m t) -> p t m", t=R))
+            return t
+
+        x_plane = tile("x_plane", [P, T], U8)
+        w1_plane = tile("w1_plane", [P, C], U8)
+        w2_plane = tile("w2_plane", [P, C], U8)
+        w34_plane = tile("w34_plane", [P, C], U8)
+        nc.vector.memset(w1_plane[:].bitcast(I32), 0)
+        nc.vector.memset(w2_plane[:].bitcast(I32), 0)
+        nc.vector.memset(w34_plane[:].bitcast(I32), 0)
+
+        offs_t = load_list("offs_t", offs)
+        for q in range(4):
+            nc.sync.dma_start(x_plane[32 * q : 32 * q + 32, :].bitcast(I32), x_scales[0, 4 * q : 4 * q + 4, :].bitcast(I32).partition_broadcast(8))
+        hz_t = load_list("hz_t", hz)
+        w1_raw = load_words("w1_raw", w1_words, C)
+        x_table = load_words("x_table", x_words, T)
+        load_scale_rows(nc.sync, w1_plane, 0, w1_scales)
+        n1_t = load_list("n1_t", n1)
+        sl_t = load_vec(nc.gpsimd, "sl_t", sl)
+        w2_raw = load_words("w2_raw", w2_words, C)
+        load_scale_rows(nc.sync, w2_plane, 0, w2_scales)
+
+        yh_win = [tile(f"yh_win{t}", [P, WIN], F32) for t in range(R)]
+        d_win = [tile(f"d_win{t}", [P, WIN], F32) for t in range(R)]
+        for win in yh_win + d_win:
+            nc.vector.memset(win[:, S:], 0.0)
+
+        xs_offs = tile("xs_offs", [P, S], U8)
+        xs_hz_raw = tile("xs_hz_raw", [P, S], U8)
+        xs_hz = tile("xs_hz", [P, S], U8)
+        nc.vector.tensor_copy(xs_hz_raw[:], x_plane[:].indirect(hz_t[:]))
+        nc.vector.tensor_copy(xs_hz[:].bitcast(I32), xs_hz_raw[:].bitcast(I32))
+        for r in (2, 3):
+            nc.sync.dma_start(xs_hz[r:P:32, :].bitcast(I32), xs_hz_raw[16 + r : P : 32, :].bitcast(I32))
+        nc.vector.tensor_copy(xs_offs[:], x_plane[:].indirect(offs_t[:]))
+
+        n2_t = load_list("n2_t", n2)
+        gn_t = load_vec(nc.gpsimd, "gn_t", gn)
+        gm_t = load_vec(nc.gpsimd, "gm_t", gm)
+        n3_t = load_list("n3_t", n3)
+        n4_t = load_list("n4_t", n4)
+        w3_raw = load_words("w3_raw", w3_words, C)
+        w4_raw = load_words("w4_raw", w4_words, C)
+        load_scale_rows(nc.sync, w34_plane, 0, w3_scales)
+        load_scale_rows(nc.sync, w34_plane, 4, w4_scales)
+        n5_t = load_list("n5_t", n5)
+        tau_t = load_vec(nc.gpsimd, "tau_t", tau)
+
+        w1 = deal(nc.scalar.copy, "w1", w1_raw, U32)
+        w1_s = deal(nc.vector.tensor_copy, "w1_s", w1_plane, U8)
+        w2 = deal(nc.scalar.copy, "w2", w2_raw, U32)
+
+        x_offs = tile("x_offs", [P, S], U32)
+        x_hz = tile("x_hz", [P, S], U32)
+        nc.vector.tensor_copy(x_offs[:], x_table[:].indirect(offs_t[:]))
+        nc.vector.tensor_copy(x_hz[:], x_table[:].indirect(hz_t[:]))
+        w2_s = deal(nc.vector.tensor_copy, "w2_s", w2_plane, U8)
+
+        def mm(out, w, w_s, first, t, rhs, rhs_s, start, stop):
+            cols = slice(P * t, P * (t + 1))
+            nc.tensor.matmul_mx(out=out, lhsT=w[:, cols].bitcast(FP8X4), lhsT_scale=w_s[first:P, cols],
+                                rhs=rhs.bitcast(FP8X4), rhs_scale=rhs_s, start=start, stop=stop)
+
+        y_ps = [psum.tile([P, S], F32, name=f"y_ps{t}", tag=f"bank{t}") for t in range(R)]
+        d_ps = [psum.tile([P, S], F32, name=f"d_ps{t}", tag=f"bank{R + t}") for t in range(R)]
+        for t in range(R):
+            mm(y_ps[t][:], w1, w1_s, 0, t, x_offs[:], xs_offs[:], True, True)
+        for t in range(R):
+            mm(d_ps[t][:], w2, w2_s, 0, t, x_hz[:], xs_hz[:], True, True)
+
+        y_sum = tile("y_sum", [P, R], F32)
+        sg_bias = tile("sg_bias", [P, R], F32)
+        sg = tile("sg", [P, R, S], F32)
+        for t in range(R):
+            nc.vector.tensor_scalar(yh_win[t][:, :S], y_ps[t][:], 1.0, None, ALU.mult, ALU.add, accum_out=y_sum[:, t : t + 1])
+            nc.vector.tensor_scalar(sg_bias[:, t : t + 1], y_sum[:, t : t + 1], -1.0 / S, sl_t[:, t : t + 1], ALU.mult, ALU.mult)
+            nc.scalar.activation(sg[:, t, :], yh_win[t][:].indirect(n1_t[:]), ACT.Sigmoid,
+                                 bias=sg_bias[:, t : t + 1], scale=sl_t[:, t : t + 1])
+        for t in range(R):
+            nc.vector.tensor_copy(d_win[t][:, :S], d_ps[t][:])
+
+        d2 = tile("d2", [P, R, S], F32)
+        d3 = tile("d3", [P, R, S], F32)
+        d4 = tile("d4", [P, R, S], F32)
+        for t in range(R):
+            nc.scalar.activation(d2[:, t, :], d_win[t][:].indirect(n2_t[:]), ACT.Copy)
+        for t in range(R):
+            nc.scalar.activation(d3[:, t, :], d_win[t][:].indirect(n3_t[:]), ACT.Copy)
+        for half in range(2):
+            cols = slice(HALF * half, HALF * (half + 1))
+            for t in range(R):
+                nc.scalar.activation(d4[:, t, cols], d_win[t][:].indirect(n4_t[:, 8 * half : 8 * half + 8]), ACT.Copy)
+
+        neg_mu = tile("neg_mu", [P, R], F32)
+        g2 = tile("g2", [P, R], F32)
+        yc = tile("yc", [P, R, S], F32)
+        nc.vector.tensor_scalar(neg_mu[:], y_sum[:], -1.0 / S, None, ALU.mult)
+        nc.vector.tensor_scalar(g2[:], gm_t[:], 0.75, None, ALU.mult)
+        for t in range(R):
+            nc.vector.tensor_scalar(yc[:, t, :], yh_win[t][:, :S], neg_mu[:, t : t + 1], gn_t[:, t : t + 1], ALU.add, ALU.mult)
+
+        def woven(bf):
+            return bf.rearrange("p (c i t) -> p c t i", i=4, t=R)
+
+        def planar(f):
+            return f.rearrange("p t (c i) -> p c t i", i=4)
+
+        z_bf = tile("z_bf", [P, R * S], BF16)
+        z_words = tile("z_words", [P, S], U32)
+        z_s = tile("z_s", [P, S], U8)
+        nc.vector.tensor_tensor(woven(z_bf[:]), planar(yc[:]), planar(sg[:]), ALU.mult)
+        pa = tile("pa", [P, R, S], F32)
+        pb = tile("pb", [P, R, S], F32)
+        nc.vector.scalar_tensor_tensor(pa[:, 0, :], d_win[0][:, :S], g2[:, 0:1], d2[:, 0, :], ALU.mult, ALU.mult)
+        nc.vector.quantize_mx(out=z_words[:].bitcast(FP8X4), scales=z_s[:], in_=z_bf[:])
+        for t in range(1, R):
+            nc.vector.scalar_tensor_tensor(pa[:, t, :], d_win[t][:, :S], g2[:, t : t + 1], d2[:, t, :], ALU.mult, ALU.mult)
+
+        w3 = deal(nc.vector.tensor_copy, "w3", w3_raw, U32)
+        w4 = deal(nc.vector.tensor_copy, "w4", w4_raw, U32)
+        w34_s = deal(nc.vector.tensor_copy, "w34_s", w34_plane, U8)
+
+        h_ps = [psum.tile([P, S], F32, name=f"h_ps{t}", tag=f"bank{t}") for t in range(R)]
+        for t in range(R):
+            mm(h_ps[t][:], w3, w34_s, 0, t, z_words[:], z_s[:], True, False)
+
+        for half in range(2):
+            cols = slice(HALF * half, HALF * (half + 1))
+            z2_bf = tile(f"z2_bf{half}", [P, R * HALF], BF16)
+            z2_words = tile(f"z2_words{half}", [P, HALF], U32)
+            z2_s = tile(f"z2_s{half}", [P, HALF], U8)
+            for t in range(R):
+                nc.vector.scalar_tensor_tensor(pb[:, t, cols], d3[:, t, cols], g2[:, t : t + 1], d4[:, t, cols], ALU.mult, ALU.mult)
+            nc.vector.tensor_tensor(woven(z2_bf[:]), planar(pa[:, :, cols]), planar(pb[:, :, cols]), ALU.add)
+            nc.vector.quantize_mx(out=z2_words[:].bitcast(FP8X4), scales=z2_s[:], in_=z2_bf[:])
+            for t in range(R):
+                mm(h_ps[t][:, cols], w4, w34_s, 4, t, z2_words[:], z2_s[:], False, half == 1)
+
+        top = tile("top", [P, R], F32)
+        ea_bias = tile("ea_bias", [P, R], F32)
+        for t in range(R):
+            nc.vector.tensor_scalar(yh_win[t][:, :S], h_ps[t][:], 1.0, None, ALU.mult, ALU.max, accum_out=top[:, t : t + 1])
+            nc.vector.tensor_scalar(ea_bias[:, t : t + 1], top[:, t : t + 1], -1.0, tau_t[:, t : t + 1], ALU.mult, ALU.mult)
+
+        o_words = tile("o_words", [P, S], U32)
+        o_s = tile("o_s", [P, S], U8)
+        out_rows = out_0.rearrange("(p t) j -> p t j", t=R)
+        units = [(half, t) for half in range(2) for t in range(R)]
+        o_f = [tile(f"o_f{half}", [P, R, HALF], F32) for half in range(2)]
+        ea, hi, lo, mx, mn, gap = {}, {}, {}, {}, {}, {}
+
+        def gather(u):
+            half, t = u
+            ea[u] = tile(f"ea{half}{t}", [P, HALF, 4], F32)
+            flat = ea[u][:].rearrange("p j m -> p (j m)")
+            for piece in range(2):
+                c0 = 32 * half + 16 * piece
+                nc.scalar.activation(flat[:, S * piece : S * (piece + 1)], yh_win[t][:].indirect(n5_t[:, c0 : c0 + 16]), ACT.Exp,
+                                     bias=ea_bias[:, t : t + 1], scale=tau_t[:, t : t + 1])
+
+        def pairs(u, store, op, name):
+            store[u] = tile(f"{name}{u[0]}{u[1]}", [P, HALF, 2], F32)
+            nc.vector.tensor_tensor(store[u][:], ea[u][:, :, 0:2], ea[u][:, :, 2:4], op)
+
+        def fold(u, store, src, op, name):
+            store[u] = tile(f"{name}{u[0]}{u[1]}", [P, HALF], F32)
+            nc.vector.tensor_tensor(store[u][:], src[u][:, :, 0], src[u][:, :, 1], op)
+
+        def spread(u):
+            gap[u] = tile(f"gap{u[0]}{u[1]}", [P, HALF], F32)
+            nc.vector.tensor_tensor(gap[u][:], mx[u][:], mn[u][:], ALU.subtract)
+
+        def finish(u):
+            half, t = u
+            nc.vector.scalar_tensor_tensor(o_f[half][:, t, :], gap[u][:], 3.0, yh_win[t][:, HALF * half : HALF * (half + 1)], ALU.mult, ALU.mult)
+
+        def hand_out(half, copy):
+            cols = slice(HALF * half, HALF * (half + 1))
+            o_bf = tile(f"o_bf{half}", [P, R * HALF], BF16)
+            nc.sync.dma_start(out_rows[:, :, cols], o_f[half][:])
+            copy(woven(o_bf[:]), planar(o_f[half][:]))
+            nc.vector.quantize_mx(out=o_words[:, cols].bitcast(FP8X4), scales=o_s[:, cols], in_=o_bf[:])
+            nc.sync.dma_start(out_1[0].rearrange("p n t -> p (n t)").bitcast(I32)[:, cols], o_words[:, cols].bitcast(I32))
+
+        for u in units:
+            gather(u)
+        for k, u in enumerate(units):
+            before = units[k - 1] if k else None
+            pairs(u, hi, ALU.max, "hi")
+            if before:
+                spread(before)
+            pairs(u, lo, ALU.min, "lo")
+            if before:
+                finish(before)
+            fold(u, mx, hi, ALU.max, "mx")
+            fold(u, mn, lo, ALU.min, "mn")
+            if u == (1, 1):
+                hand_out(0, nc.scalar.copy)
+        spread(units[-1])
+        finish(units[-1])
+        hand_out(1, nc.vector.tensor_copy)
+        for q in range(4):
+            nc.scalar.dma_start(out_2[0, 4 * q : 4 * q + 4, :].bitcast(I32), o_s[32 * q : 32 * q + 4, :].bitcast(I32))

@@ -32,16 +32,16 @@ def tile_picked_hjoinecndotegp_none_po_kernel(
         keep = ctx.enter_context(tc.tile_pool(name="keep", bufs=1))
         psum = ctx.enter_context(tc.psum_pool(name="psum", bufs=1))
 
-        def tile(name, shape, dtype):
-            return keep.tile(shape, dtype, name=name, align_bytes=64)
+        def tile(name, shape, dtype, tag=None):
+            return keep.tile(shape, dtype, name=name, tag=tag or name, align_bytes=64)
 
         def load_list(name, src):
             t = keep.tile([P, src.shape[1]], U16, name=name)
             nc.sync.dma_start(t[:], src)
             return t
 
-        def load_words(name, src, width):
-            t = tile(name, [P, width], U32)
+        def load_words(name, src, width, tag=None):
+            t = tile(name, [P, width], U32, tag)
             nc.sync.dma_start(t[:].bitcast(I32), src[0].rearrange("p n t -> p (n t)").bitcast(I32))
             return t
 
@@ -54,18 +54,16 @@ def tile_picked_hjoinecndotegp_none_po_kernel(
             queue.dma_start(t[:], src.rearrange("(p t) o -> p (t o)", t=R))
             return t
 
-        def deal(copy, name, src, dtype):
-            t = tile(name, [P, C], dtype)
-            copy(t[:].rearrange("p (t m) -> p t m", t=R), src[:].rearrange("p (m t) -> p t m", t=R))
+        def deal(copy, name, src, dtype, tag=None):
+            t = tile(name, [P, C], dtype, tag)
+            copy(t[:].rearrange("p (t m) -> p m t", t=R), src[:].rearrange("p (m t) -> p m t", t=R))
             return t
 
         x_plane = tile("x_plane", [P, T], U8)
         w1_plane = tile("w1_plane", [P, C], U8)
         w2_plane = tile("w2_plane", [P, C], U8)
-        w34_plane = tile("w34_plane", [P, C], U8)
         nc.vector.memset(w1_plane[:].bitcast(I32), 0)
         nc.vector.memset(w2_plane[:].bitcast(I32), 0)
-        nc.vector.memset(w34_plane[:].bitcast(I32), 0)
 
         offs_t = load_list("offs_t", offs)
         for q in range(4):
@@ -75,9 +73,12 @@ def tile_picked_hjoinecndotegp_none_po_kernel(
         x_table = load_words("x_table", x_words, T)
         load_scale_rows(nc.sync, w1_plane, 0, w1_scales)
         n1_t = load_list("n1_t", n1)
-        sl_t = load_vec(nc.gpsimd, "sl_t", sl)
         w2_raw = load_words("w2_raw", w2_words, C)
+        sl_t = load_vec(nc.gpsimd, "sl_t", sl)
         load_scale_rows(nc.sync, w2_plane, 0, w2_scales)
+        gn_t = load_vec(nc.gpsimd, "gn_t", gn)
+        gm_t = load_vec(nc.gpsimd, "gm_t", gm)
+        tau_t = load_vec(nc.gpsimd, "tau_t", tau)
 
         yh_win = [tile(f"yh_win{t}", [P, WIN], F32) for t in range(R)]
         d_win = [tile(f"d_win{t}", [P, WIN], F32) for t in range(R)]
@@ -94,26 +95,25 @@ def tile_picked_hjoinecndotegp_none_po_kernel(
         nc.vector.tensor_copy(xs_offs[:], x_plane[:].indirect(offs_t[:]))
 
         n2_t = load_list("n2_t", n2)
-        gn_t = load_vec(nc.gpsimd, "gn_t", gn)
-        gm_t = load_vec(nc.gpsimd, "gm_t", gm)
         n3_t = load_list("n3_t", n3)
         n4_t = load_list("n4_t", n4)
-        w3_raw = load_words("w3_raw", w3_words, C)
-        w4_raw = load_words("w4_raw", w4_words, C)
-        load_scale_rows(nc.sync, w34_plane, 0, w3_scales)
-        load_scale_rows(nc.sync, w34_plane, 4, w4_scales)
         n5_t = load_list("n5_t", n5)
-        tau_t = load_vec(nc.gpsimd, "tau_t", tau)
 
         w1 = deal(nc.scalar.copy, "w1", w1_raw, U32)
-        w1_s = deal(nc.vector.tensor_copy, "w1_s", w1_plane, U8)
         w2 = deal(nc.scalar.copy, "w2", w2_raw, U32)
+        w1_s = deal(nc.vector.tensor_copy, "w1_s", w1_plane, U8)
+        w34_raw = tile("w34_raw", [P, 2 * C], U32, "w1_raw")
+        w3_raw, w4_raw = w34_raw[:, :C], w34_raw[:, C:]
+        for dst, src in ((w3_raw, w3_words), (w4_raw, w4_words)):
+            nc.sync.dma_start(dst.bitcast(I32), src[0].rearrange("p n t -> p (n t)").bitcast(I32))
+        w34_plane = w1_plane
+        load_scale_rows(nc.sync, w34_plane, 0, w3_scales)
+        load_scale_rows(nc.sync, w34_plane, 4, w4_scales)
 
         x_offs = tile("x_offs", [P, S], U32)
         x_hz = tile("x_hz", [P, S], U32)
         nc.vector.tensor_copy(x_offs[:], x_table[:].indirect(offs_t[:]))
         nc.vector.tensor_copy(x_hz[:], x_table[:].indirect(hz_t[:]))
-        w2_s = deal(nc.vector.tensor_copy, "w2_s", w2_plane, U8)
 
         def mm(out, w, w_s, first, t, rhs, rhs_s, start, stop):
             cols = slice(P * t, P * (t + 1))
@@ -124,8 +124,6 @@ def tile_picked_hjoinecndotegp_none_po_kernel(
         d_ps = [psum.tile([P, S], F32, name=f"d_ps{t}", tag=f"bank{R + t}") for t in range(R)]
         for t in range(R):
             mm(y_ps[t][:], w1, w1_s, 0, t, x_offs[:], xs_offs[:], True, True)
-        for t in range(R):
-            mm(d_ps[t][:], w2, w2_s, 0, t, x_hz[:], xs_hz[:], True, True)
 
         y_sum = tile("y_sum", [P, R], F32)
         sg_bias = tile("sg_bias", [P, R], F32)
@@ -135,6 +133,9 @@ def tile_picked_hjoinecndotegp_none_po_kernel(
             nc.vector.tensor_scalar(sg_bias[:, t : t + 1], y_sum[:, t : t + 1], -1.0 / S, sl_t[:, t : t + 1], ALU.mult, ALU.mult)
             nc.scalar.activation(sg[:, t, :], yh_win[t][:].indirect(n1_t[:]), ACT.Sigmoid,
                                  bias=sg_bias[:, t : t + 1], scale=sl_t[:, t : t + 1])
+        w2_s = deal(nc.vector.tensor_copy, "w2_s", w2_plane, U8, "w1_s")
+        for t in range(R):
+            mm(d_ps[t][:], w2, w2_s, 0, t, x_hz[:], xs_hz[:], True, True)
         for t in range(R):
             nc.vector.tensor_copy(d_win[t][:, :S], d_ps[t][:])
 
@@ -142,21 +143,19 @@ def tile_picked_hjoinecndotegp_none_po_kernel(
         d3 = tile("d3", [P, R, S], F32)
         d4 = tile("d4", [P, R, S], F32)
         for t in range(R):
-            nc.scalar.activation(d2[:, t, :], d_win[t][:].indirect(n2_t[:]), ACT.Copy)
+            nc.scalar.activation(d2[:, t, :], d_win[t][:].indirect(n2_t[:]), ACT.Copy, scale=0.75)
         for t in range(R):
             nc.scalar.activation(d3[:, t, :], d_win[t][:].indirect(n3_t[:]), ACT.Copy)
         for half in range(2):
             cols = slice(HALF * half, HALF * (half + 1))
             for t in range(R):
-                nc.scalar.activation(d4[:, t, cols], d_win[t][:].indirect(n4_t[:, 8 * half : 8 * half + 8]), ACT.Copy)
+                nc.scalar.activation(d4[:, t, cols], d_win[t][:].indirect(n4_t[:, 8 * half : 8 * half + 8]), ACT.Copy, scale=0.75)
 
         neg_mu = tile("neg_mu", [P, R], F32)
-        g2 = tile("g2", [P, R], F32)
         yc = tile("yc", [P, R, S], F32)
-        nc.vector.tensor_scalar(neg_mu[:], y_sum[:], -1.0 / S, None, ALU.mult)
-        nc.vector.tensor_scalar(g2[:], gm_t[:], 0.75, None, ALU.mult)
+        nc.gpsimd.tensor_scalar(neg_mu[:], y_sum[:], -1.0 / S, 0.0, ALU.mult, ALU.add)
         for t in range(R):
-            nc.vector.tensor_scalar(yc[:, t, :], yh_win[t][:, :S], neg_mu[:, t : t + 1], gn_t[:, t : t + 1], ALU.add, ALU.mult)
+            nc.gpsimd.tensor_scalar(yc[:, t, :], yh_win[t][:, :S], neg_mu[:, t : t + 1], gn_t[:, t : t + 1], ALU.add, ALU.mult)
 
         def woven(bf):
             return bf.rearrange("p (c i t) -> p c t i", i=4, t=R)
@@ -164,24 +163,23 @@ def tile_picked_hjoinecndotegp_none_po_kernel(
         def planar(f):
             return f.rearrange("p t (c i) -> p c t i", i=4)
 
-        z_bf = tile("z_bf", [P, R * S], BF16)
+        z_bf = tile("z_bf", [P, R * S], BF16, "w2")
         z_words = tile("z_words", [P, S], U32)
         z_s = tile("z_s", [P, S], U8)
         nc.vector.tensor_tensor(woven(z_bf[:]), planar(yc[:]), planar(sg[:]), ALU.mult)
         pa = tile("pa", [P, R, S], F32)
         pb = tile("pb", [P, R, S], F32)
-        nc.vector.scalar_tensor_tensor(pa[:, 0, :], d_win[0][:, :S], g2[:, 0:1], d2[:, 0, :], ALU.mult, ALU.mult)
+        nc.vector.scalar_tensor_tensor(pa[:, 0, :], d_win[0][:, :S], gm_t[:, 0:1], d2[:, 0, :], ALU.mult, ALU.mult)
         nc.vector.quantize_mx(out=z_words[:].bitcast(FP8X4), scales=z_s[:], in_=z_bf[:])
         for t in range(1, R):
-            nc.vector.scalar_tensor_tensor(pa[:, t, :], d_win[t][:, :S], g2[:, t : t + 1], d2[:, t, :], ALU.mult, ALU.mult)
+            nc.vector.scalar_tensor_tensor(pa[:, t, :], d_win[t][:, :S], gm_t[:, t : t + 1], d2[:, t, :], ALU.mult, ALU.mult)
 
-        w3 = deal(nc.vector.tensor_copy, "w3", w3_raw, U32)
-        w4 = deal(nc.vector.tensor_copy, "w4", w4_raw, U32)
-        w34_s = deal(nc.vector.tensor_copy, "w34_s", w34_plane, U8)
+        w34 = tile("w34", [P, 2 * C], U32, "w1_s")
+        nc.vector.tensor_copy(w34[:].rearrange("p (w t m) -> p w m t", w=2, t=R), w34_raw[:].rearrange("p (w m t) -> p w m t", w=2, t=R))
+        w3, w4 = w34[:, :C], w34[:, C:]
+        w34_s = deal(nc.vector.tensor_copy, "w34_s", w34_plane, U8, "w2")
 
         h_ps = [psum.tile([P, S], F32, name=f"h_ps{t}", tag=f"bank{t}") for t in range(R)]
-        for t in range(R):
-            mm(h_ps[t][:], w3, w34_s, 0, t, z_words[:], z_s[:], True, False)
 
         for half in range(2):
             cols = slice(HALF * half, HALF * (half + 1))
@@ -189,11 +187,12 @@ def tile_picked_hjoinecndotegp_none_po_kernel(
             z2_words = tile(f"z2_words{half}", [P, HALF], U32)
             z2_s = tile(f"z2_s{half}", [P, HALF], U8)
             for t in range(R):
-                nc.vector.scalar_tensor_tensor(pb[:, t, cols], d3[:, t, cols], g2[:, t : t + 1], d4[:, t, cols], ALU.mult, ALU.mult)
+                nc.vector.scalar_tensor_tensor(pb[:, t, cols], d3[:, t, cols], gm_t[:, t : t + 1], d4[:, t, cols], ALU.mult, ALU.mult)
             nc.vector.tensor_tensor(woven(z2_bf[:]), planar(pa[:, :, cols]), planar(pb[:, :, cols]), ALU.add)
             nc.vector.quantize_mx(out=z2_words[:].bitcast(FP8X4), scales=z2_s[:], in_=z2_bf[:])
             for t in range(R):
-                mm(h_ps[t][:, cols], w4, w34_s, 4, t, z2_words[:], z2_s[:], False, half == 1)
+                mm(h_ps[t][:, cols], w3, w34_s, 0, t, z_words[:, cols], z_s[:, cols], True, False)
+                mm(h_ps[t][:, cols], w4, w34_s, 4, t, z2_words[:], z2_s[:], False, True)
 
         top = tile("top", [P, R], F32)
         ea_bias = tile("ea_bias", [P, R], F32)
@@ -204,34 +203,40 @@ def tile_picked_hjoinecndotegp_none_po_kernel(
         o_words = tile("o_words", [P, S], U32)
         o_s = tile("o_s", [P, S], U8)
         out_rows = out_0.rearrange("(p t) j -> p t j", t=R)
-        units = [(half, t) for half in range(2) for t in range(R)]
+        units = [(0, 0, 1), (0, 1, 2), (0, 2, 4), (1, 0, 2), (1, 2, 4)]
         o_f = [tile(f"o_f{half}", [P, R, HALF], F32) for half in range(2)]
-        ea, hi, lo, mx, mn, gap = {}, {}, {}, {}, {}, {}
+        ea = [tile(f"ea{half}", [P, R, HALF * 4], F32) for half in range(2)]
+        hi = [tile(f"hi{half}", [P, R * HALF, 2], F32) for half in range(2)]
+        lo = [tile(f"lo{half}", [P, R * HALF, 2], F32) for half in range(2)]
+        mx = [tile(f"mx{half}", [P, R * HALF], F32) for half in range(2)]
+        mn = [tile(f"mn{half}", [P, R * HALF], F32) for half in range(2)]
+        gap = [tile(f"gap{half}", [P, R * HALF], F32) for half in range(2)]
 
-        def gather(u):
-            half, t = u
-            ea[u] = tile(f"ea{half}{t}", [P, HALF, 4], F32)
-            flat = ea[u][:].rearrange("p j m -> p (j m)")
-            for piece in range(2):
-                c0 = 32 * half + 16 * piece
-                nc.scalar.activation(flat[:, S * piece : S * (piece + 1)], yh_win[t][:].indirect(n5_t[:, c0 : c0 + 16]), ACT.Exp,
-                                     bias=ea_bias[:, t : t + 1], scale=tau_t[:, t : t + 1])
+        for half in range(2):
+            for t in range(R):
+                for piece in range(2):
+                    c0 = 32 * half + 16 * piece
+                    nc.scalar.activation(ea[half][:, t, S * piece : S * (piece + 1)], yh_win[t][:].indirect(n5_t[:, c0 : c0 + 16]), ACT.Exp,
+                                         bias=ea_bias[:, t : t + 1], scale=tau_t[:, t : t + 1])
 
-        def pairs(u, store, op, name):
-            store[u] = tile(f"{name}{u[0]}{u[1]}", [P, HALF, 2], F32)
-            nc.vector.tensor_tensor(store[u][:], ea[u][:, :, 0:2], ea[u][:, :, 2:4], op)
+        def span(u):
+            return slice(HALF * u[1], HALF * u[2])
 
-        def fold(u, store, src, op, name):
-            store[u] = tile(f"{name}{u[0]}{u[1]}", [P, HALF], F32)
-            nc.vector.tensor_tensor(store[u][:], src[u][:, :, 0], src[u][:, :, 1], op)
+        def pairs(u, dst, op):
+            members = ea[u[0]][:].rearrange("p t (j m) -> p (t j) m", m=4)
+            nc.vector.tensor_tensor(dst[u[0]][:, span(u), :], members[:, span(u), 0:2], members[:, span(u), 2:4], op)
+
+        def fold(u, dst, src, op):
+            nc.vector.tensor_tensor(dst[u[0]][:, span(u)], src[u[0]][:, span(u), 0], src[u[0]][:, span(u), 1], op)
 
         def spread(u):
-            gap[u] = tile(f"gap{u[0]}{u[1]}", [P, HALF], F32)
-            nc.vector.tensor_tensor(gap[u][:], mx[u][:], mn[u][:], ALU.subtract)
+            nc.vector.tensor_tensor(gap[u[0]][:, span(u)], mx[u[0]][:, span(u)], mn[u[0]][:, span(u)], ALU.subtract)
 
         def finish(u):
-            half, t = u
-            nc.vector.scalar_tensor_tensor(o_f[half][:, t, :], gap[u][:], 3.0, yh_win[t][:, HALF * half : HALF * (half + 1)], ALU.mult, ALU.mult)
+            half = u[0]
+            for t in range(u[1], u[2]):
+                nc.vector.scalar_tensor_tensor(o_f[half][:, t, :], gap[half][:, HALF * t : HALF * (t + 1)], 3.0,
+                                               yh_win[t][:, HALF * half : HALF * (half + 1)], ALU.mult, ALU.mult)
 
         def hand_out(half, copy):
             cols = slice(HALF * half, HALF * (half + 1))
@@ -241,19 +246,17 @@ def tile_picked_hjoinecndotegp_none_po_kernel(
             nc.vector.quantize_mx(out=o_words[:, cols].bitcast(FP8X4), scales=o_s[:, cols], in_=o_bf[:])
             nc.sync.dma_start(out_1[0].rearrange("p n t -> p (n t)").bitcast(I32)[:, cols], o_words[:, cols].bitcast(I32))
 
-        for u in units:
-            gather(u)
         for k, u in enumerate(units):
             before = units[k - 1] if k else None
-            pairs(u, hi, ALU.max, "hi")
+            pairs(u, hi, ALU.max)
             if before:
                 spread(before)
-            pairs(u, lo, ALU.min, "lo")
+            pairs(u, lo, ALU.min)
             if before:
                 finish(before)
-            fold(u, mx, hi, ALU.max, "mx")
-            fold(u, mn, lo, ALU.min, "mn")
-            if u == (1, 1):
+            fold(u, mx, hi, ALU.max)
+            fold(u, mn, lo, ALU.min)
+            if k == len(units) - 1:
                 hand_out(0, nc.scalar.copy)
         spread(units[-1])
         finish(units[-1])

@@ -101,7 +101,10 @@ def tile_picked_hjoinecndotegp_none_po_kernel(
 
         w1 = deal(nc.scalar.copy, "w1", w1_raw, U32)
         w2 = deal(nc.scalar.copy, "w2", w2_raw, U32)
-        w1_s = deal(nc.vector.tensor_copy, "w1_s", w1_plane, U8)
+        w1_s = tile("w1_s", [P, C], U8)
+        by_tile = w1_plane[:].rearrange("p (m t) -> p m t", t=R)
+        nc.vector.tensor_copy(w1_s[:, :P], by_tile[:, :, 0])
+        nc.vector.tensor_copy(w1_s[:, P:].rearrange("p (t m) -> p m t", t=R - 1), by_tile[:, :, 1:])
         w34_raw = tile("w34_raw", [P, 2 * C], U32, "w1_raw")
         w3_raw, w4_raw = w34_raw[:, :C], w34_raw[:, C:]
         for dst, src in ((w3_raw, w3_words), (w4_raw, w4_words)):
@@ -130,7 +133,7 @@ def tile_picked_hjoinecndotegp_none_po_kernel(
         sg = tile("sg", [P, R, S], F32)
         for t in range(R):
             nc.vector.tensor_scalar(yh_win[t][:, :S], y_ps[t][:], 1.0, None, ALU.mult, ALU.add, accum_out=y_sum[:, t : t + 1])
-            nc.vector.tensor_scalar(sg_bias[:, t : t + 1], y_sum[:, t : t + 1], -1.0 / S, sl_t[:, t : t + 1], ALU.mult, ALU.mult)
+            nc.gpsimd.tensor_scalar(sg_bias[:, t : t + 1], y_sum[:, t : t + 1], -1.0 / S, sl_t[:, t : t + 1], ALU.mult, ALU.mult)
             nc.scalar.activation(sg[:, t, :], yh_win[t][:].indirect(n1_t[:]), ACT.Sigmoid,
                                  bias=sg_bias[:, t : t + 1], scale=sl_t[:, t : t + 1])
         w2_s = deal(nc.vector.tensor_copy, "w2_s", w2_plane, U8, "w1_s")
@@ -168,7 +171,6 @@ def tile_picked_hjoinecndotegp_none_po_kernel(
         z_s = tile("z_s", [P, S], U8)
         nc.vector.tensor_tensor(woven(z_bf[:]), planar(yc[:]), planar(sg[:]), ALU.mult)
         pa = tile("pa", [P, R, S], F32)
-        pb = tile("pb", [P, R, S], F32)
         nc.vector.scalar_tensor_tensor(pa[:, 0, :], d_win[0][:, :S], gm_t[:, 0:1], d2[:, 0, :], ALU.mult, ALU.mult)
         nc.vector.quantize_mx(out=z_words[:].bitcast(FP8X4), scales=z_s[:], in_=z_bf[:])
         for t in range(1, R):
@@ -180,37 +182,40 @@ def tile_picked_hjoinecndotegp_none_po_kernel(
         w34_s = deal(nc.vector.tensor_copy, "w34_s", w34_plane, U8, "w2")
 
         h_ps = [psum.tile([P, S], F32, name=f"h_ps{t}", tag=f"bank{t}") for t in range(R)]
+        for t in range(R):
+            mm(h_ps[t][:], w3, w34_s, 0, t, z_words[:], z_s[:], True, False)
 
         for half in range(2):
             cols = slice(HALF * half, HALF * (half + 1))
             z2_bf = tile(f"z2_bf{half}", [P, R * HALF], BF16)
+            pb = tile(f"pb{half}", [P, R, HALF], F32, "z2_bf0" if half else "w1_plane")
             z2_words = tile(f"z2_words{half}", [P, HALF], U32)
             z2_s = tile(f"z2_s{half}", [P, HALF], U8)
             for t in range(R):
-                nc.vector.scalar_tensor_tensor(pb[:, t, cols], d3[:, t, cols], gm_t[:, t : t + 1], d4[:, t, cols], ALU.mult, ALU.mult)
-            nc.vector.tensor_tensor(woven(z2_bf[:]), planar(pa[:, :, cols]), planar(pb[:, :, cols]), ALU.add)
+                nc.vector.scalar_tensor_tensor(pb[:, t, :], d3[:, t, cols], gm_t[:, t : t + 1], d4[:, t, cols], ALU.mult, ALU.mult)
+            nc.vector.tensor_tensor(woven(z2_bf[:]), planar(pa[:, :, cols]), planar(pb[:]), ALU.add)
             nc.vector.quantize_mx(out=z2_words[:].bitcast(FP8X4), scales=z2_s[:], in_=z2_bf[:])
             for t in range(R):
-                mm(h_ps[t][:, cols], w3, w34_s, 0, t, z_words[:, cols], z_s[:, cols], True, False)
-                mm(h_ps[t][:, cols], w4, w34_s, 4, t, z2_words[:], z2_s[:], False, True)
+                mm(h_ps[t][:, cols], w4, w34_s, 4, t, z2_words[:], z2_s[:], False, half == 1)
 
         top = tile("top", [P, R], F32)
         ea_bias = tile("ea_bias", [P, R], F32)
         for t in range(R):
             nc.vector.tensor_scalar(yh_win[t][:, :S], h_ps[t][:], 1.0, None, ALU.mult, ALU.max, accum_out=top[:, t : t + 1])
-            nc.vector.tensor_scalar(ea_bias[:, t : t + 1], top[:, t : t + 1], -1.0, tau_t[:, t : t + 1], ALU.mult, ALU.mult)
+            nc.gpsimd.tensor_scalar(ea_bias[:, t : t + 1], top[:, t : t + 1], -1.0, tau_t[:, t : t + 1], ALU.mult, ALU.mult)
 
         o_words = tile("o_words", [P, S], U32)
         o_s = tile("o_s", [P, S], U8)
         out_rows = out_0.rearrange("(p t) j -> p t j", t=R)
-        units = [(0, 0, 1), (0, 1, 2), (0, 2, 4), (1, 0, 2), (1, 2, 4)]
         o_f = [tile(f"o_f{half}", [P, R, HALF], F32) for half in range(2)]
         ea = [tile(f"ea{half}", [P, R, HALF * 4], F32) for half in range(2)]
-        hi = [tile(f"hi{half}", [P, R * HALF, 2], F32) for half in range(2)]
-        lo = [tile(f"lo{half}", [P, R * HALF, 2], F32) for half in range(2)]
-        mx = [tile(f"mx{half}", [P, R * HALF], F32) for half in range(2)]
-        mn = [tile(f"mn{half}", [P, R * HALF], F32) for half in range(2)]
-        gap = [tile(f"gap{half}", [P, R * HALF], F32) for half in range(2)]
+        mx = [tile(f"mx{half}", [P, R, HALF], F32) for half in range(2)]
+        mn = [tile(f"mn{half}", [P, R, HALF], F32) for half in range(2)]
+        gap = [tile(f"gap{half}", [P, R, HALF], F32) for half in range(2)]
+        h3 = tile("h3", [P, R, S], F32)
+        o_bf = tile("o_bf", [P, R * S], BF16)
+        for t in range(R):
+            nc.gpsimd.tensor_scalar(h3[:, t, :], yh_win[t][:, :S], 3.0, 0.0, ALU.mult, ALU.add)
 
         for half in range(2):
             for t in range(R):
@@ -219,47 +224,22 @@ def tile_picked_hjoinecndotegp_none_po_kernel(
                     nc.scalar.activation(ea[half][:, t, S * piece : S * (piece + 1)], yh_win[t][:].indirect(n5_t[:, c0 : c0 + 16]), ACT.Exp,
                                          bias=ea_bias[:, t : t + 1], scale=tau_t[:, t : t + 1])
 
-        def span(u):
-            return slice(HALF * u[1], HALF * u[2])
-
-        def pairs(u, dst, op):
-            members = ea[u[0]][:].rearrange("p t (j m) -> p (t j) m", m=4)
-            nc.vector.tensor_tensor(dst[u[0]][:, span(u), :], members[:, span(u), 0:2], members[:, span(u), 2:4], op)
-
-        def fold(u, dst, src, op):
-            nc.vector.tensor_tensor(dst[u[0]][:, span(u)], src[u[0]][:, span(u), 0], src[u[0]][:, span(u), 1], op)
-
-        def spread(u):
-            nc.vector.tensor_tensor(gap[u[0]][:, span(u)], mx[u[0]][:, span(u)], mn[u[0]][:, span(u)], ALU.subtract)
-
-        def finish(u):
-            half = u[0]
-            for t in range(u[1], u[2]):
-                nc.vector.scalar_tensor_tensor(o_f[half][:, t, :], gap[half][:, HALF * t : HALF * (t + 1)], 3.0,
-                                               yh_win[t][:, HALF * half : HALF * (half + 1)], ALU.mult, ALU.mult)
-
-        def hand_out(half, copy):
+        for half in range(2):
             cols = slice(HALF * half, HALF * (half + 1))
-            o_bf = tile(f"o_bf{half}", [P, R * HALF], BF16)
+            for t in range(R):
+                last = half == 1 and t == R - 1
+                members = ea[half][:, t, :].rearrange("p (j m) -> p j m", m=4)
+                for js in (slice(0, 64), slice(64, HALF)) if last else (slice(0, HALF),):
+                    nc.vector.tensor_reduce(mx[half][:, t, js], members[:, js, :], mybir.AxisListType.X, ALU.max)
+                    nc.vector.tensor_reduce(mn[half][:, t, js], members[:, js, :], mybir.AxisListType.X, ALU.min)
+                engine = nc.vector if last else nc.gpsimd
+                engine.tensor_tensor(gap[half][:, t, :], mx[half][:, t, :], mn[half][:, t, :], ALU.subtract)
+                engine.tensor_tensor(o_f[half][:, t, :], gap[half][:, t, :], h3[:, t, cols], ALU.mult)
             nc.sync.dma_start(out_rows[:, :, cols], o_f[half][:])
-            copy(woven(o_bf[:]), planar(o_f[half][:]))
-            nc.vector.quantize_mx(out=o_words[:, cols].bitcast(FP8X4), scales=o_s[:, cols], in_=o_bf[:])
-            nc.sync.dma_start(out_1[0].rearrange("p n t -> p (n t)").bitcast(I32)[:, cols], o_words[:, cols].bitcast(I32))
-
-        for k, u in enumerate(units):
-            before = units[k - 1] if k else None
-            pairs(u, hi, ALU.max)
-            if before:
-                spread(before)
-            pairs(u, lo, ALU.min)
-            if before:
-                finish(before)
-            fold(u, mx, hi, ALU.max)
-            fold(u, mn, lo, ALU.min)
-            if k == len(units) - 1:
-                hand_out(0, nc.scalar.copy)
-        spread(units[-1])
-        finish(units[-1])
-        hand_out(1, nc.vector.tensor_copy)
+            copy = nc.vector.tensor_copy if half else nc.scalar.copy
+            copy(woven(o_bf[:, R * HALF * half : R * HALF * (half + 1)]), planar(o_f[half][:]))
+        nc.vector.quantize_mx(out=o_words[:].bitcast(FP8X4), scales=o_s[:], in_=o_bf[:])
+        nc.sync.dma_start(out_1[0].rearrange("p n t -> p (n t)").bitcast(I32), o_words[:].bitcast(I32))
         for q in range(4):
-            nc.scalar.dma_start(out_2[0, 4 * q : 4 * q + 4, :].bitcast(I32), o_s[32 * q : 32 * q + 4, :].bitcast(I32))
+            queue = nc.scalar if q else nc.sync
+            queue.dma_start(out_2[0, 4 * q : 4 * q + 4, :].bitcast(I32), o_s[32 * q : 32 * q + 4, :].bitcast(I32))

@@ -11,14 +11,19 @@ U8 = mybir.dt.uint8
 FP8X4 = mybir.dt.float8_e4m3fn_x4
 ALU = mybir.AluOpType
 ACT = mybir.ActivationFunctionType
+AXIS_X = mybir.AxisListType.X
 
 P = 128
+QUADRANTS = 4
 T = 2048
 S = 256
 C = 512
 R = 4
-HALF = 128
-WIN = 512
+HALF = S // 2
+MEMBERS = 4
+LIST_ROWS = 16
+D_WIN = 2 * S
+YH_WIN = 4 * S
 FLOPS = 4 * 2 * 512 * 512 * 256
 
 
@@ -32,32 +37,54 @@ def tile_picked_hjoinecndotegp_none_po_kernel(
         keep = ctx.enter_context(tc.tile_pool(name="keep", bufs=1))
         psum = ctx.enter_context(tc.psum_pool(name="psum", bufs=1))
 
-        def tile(name, shape, dtype, tag=None):
-            return keep.tile(shape, dtype, name=name, tag=tag or name, align_bytes=64)
+        def tile(name, shape, dtype, after=None):
+            return keep.tile(shape, dtype, name=name, tag=after or name, align_bytes=64)
+
+        def as_words(planes):
+            return planes[0].rearrange("p n t -> p (n t)").bitcast(I32)
 
         def load_list(name, src):
-            t = keep.tile([P, src.shape[1]], U16, name=name)
-            nc.sync.dma_start(t[:], src)
-            return t
+            offsets = keep.tile([P, src.shape[1]], U16, name=name)
+            nc.sync.dma_start(offsets[:], src)
+            return offsets
 
-        def load_words(name, src, width, tag=None):
-            t = tile(name, [P, width], U32, tag)
-            nc.sync.dma_start(t[:].bitcast(I32), src[0].rearrange("p n t -> p (n t)").bitcast(I32))
-            return t
+        def load_words(name, src, width):
+            words = tile(name, [P, width], U32)
+            nc.sync.dma_start(words[:].bitcast(I32), as_words(src))
+            return words
 
-        def load_scale_rows(queue, plane, first, src):
-            for q in range(4):
-                queue.dma_start(plane[32 * q + first : 32 * q + first + 4, :].bitcast(I32), src[0, 4 * q : 4 * q + 4, :].bitcast(I32))
+        def load_scale_rows(plane, first, src):
+            for q in range(QUADRANTS):
+                rows = plane[32 * q + first : 32 * q + first + 4, :]
+                nc.sync.dma_start(rows.bitcast(I32), src[0, 4 * q : 4 * q + 4, :].bitcast(I32))
 
-        def load_vec(queue, name, src):
-            t = tile(name, [P, R], F32)
-            queue.dma_start(t[:], src.rearrange("(p t) o -> p (t o)", t=R))
-            return t
+        def load_per_row(queue, name, src):
+            values = tile(name, [P, R], F32)
+            queue.dma_start(values[:], src.rearrange("(p t) o -> p (t o)", t=R))
+            return values
 
-        def deal(copy, name, src, dtype, tag=None):
-            t = tile(name, [P, C], dtype, tag)
-            copy(t[:].rearrange("p (t m) -> p m t", t=R), src[:].rearrange("p (m t) -> p m t", t=R))
-            return t
+        def deal(copy, name, src, dtype, after=None):
+            dealt = tile(name, [P, C], dtype, after)
+            copy(dealt[:].rearrange("p (t m) -> p m t", t=R), src[:].rearrange("p (m t) -> p m t", t=R))
+            return dealt
+
+        def deal_first_tile_ahead(copy, name, src, dtype, after=None):
+            dealt = tile(name, [P, C], dtype, after)
+            by_tile = src[:].rearrange("p (m t) -> p m t", t=R)
+            copy(dealt[:, :P], by_tile[:, :, 0])
+            copy(dealt[:, P:].rearrange("p (t m) -> p m t", t=R - 1), by_tile[:, :, 1:])
+            return dealt
+
+        def product(out, w, w_s, first, t, rhs, rhs_s, start, stop):
+            cols = slice(P * t, P * (t + 1))
+            nc.tensor.matmul_mx(out=out, lhsT=w[:, cols].bitcast(FP8X4), lhsT_scale=w_s[first:P, cols],
+                                rhs=rhs.bitcast(FP8X4), rhs_scale=rhs_s, start=start, stop=stop)
+
+        def woven(bf):
+            return bf.rearrange("p (c i t) -> p c t i", i=4, t=R)
+
+        def planar(values):
+            return values.rearrange("p t (c i) -> p c t i", i=4)
 
         x_plane = tile("x_plane", [P, T], U8)
         w1_plane = tile("w1_plane", [P, C], U8)
@@ -66,24 +93,27 @@ def tile_picked_hjoinecndotegp_none_po_kernel(
         nc.vector.memset(w2_plane[:].bitcast(I32), 0)
 
         offs_t = load_list("offs_t", offs)
-        for q in range(4):
-            nc.sync.dma_start(x_plane[32 * q : 32 * q + 32, :].bitcast(I32), x_scales[0, 4 * q : 4 * q + 4, :].bitcast(I32).partition_broadcast(8))
+        for q in range(QUADRANTS):
+            rows = x_scales[0, 4 * q : 4 * q + 4, :].bitcast(I32)
+            nc.sync.dma_start(x_plane[32 * q : 32 * q + 32, :].bitcast(I32), rows.partition_broadcast(8))
         hz_t = load_list("hz_t", hz)
-        w1_raw = load_words("w1_raw", w1_words, C)
         x_table = load_words("x_table", x_words, T)
-        load_scale_rows(nc.sync, w1_plane, 0, w1_scales)
         n1_t = load_list("n1_t", n1)
+        load_scale_rows(w1_plane, 0, w1_scales)
+        w1_raw = load_words("w1_raw", w1_words, C)
         w2_raw = load_words("w2_raw", w2_words, C)
-        sl_t = load_vec(nc.gpsimd, "sl_t", sl)
-        load_scale_rows(nc.sync, w2_plane, 0, w2_scales)
-        gn_t = load_vec(nc.gpsimd, "gn_t", gn)
-        gm_t = load_vec(nc.gpsimd, "gm_t", gm)
-        tau_t = load_vec(nc.gpsimd, "tau_t", tau)
+        sl_t = load_per_row(nc.gpsimd, "sl_t", sl)
+        load_scale_rows(w2_plane, 0, w2_scales)
+        gn_t = load_per_row(nc.gpsimd, "gn_t", gn)
+        gm_t = load_per_row(nc.gpsimd, "gm_t", gm)
 
-        yh_win = [tile(f"yh_win{t}", [P, WIN], F32) for t in range(R)]
-        d_win = [tile(f"d_win{t}", [P, WIN], F32) for t in range(R)]
+        yh_win = [tile(f"yh_win{t}", [P, YH_WIN], F32) for t in range(R)]
+        d_win = [tile(f"d_win{t}", [P, D_WIN], F32) for t in range(R)]
         for win in yh_win + d_win:
-            nc.vector.memset(win[:, S:], 0.0)
+            nc.vector.memset(win[:, S : 2 * S], 0.0)
+        for win in yh_win:
+            zeros = win[:, S : 2 * S].unsqueeze(1).to_broadcast([P, 2, S])
+            nc.scalar.copy(win[:, 2 * S :].rearrange("p (a s) -> p a s", a=2), zeros)
 
         xs_offs = tile("xs_offs", [P, S], U8)
         xs_hz_raw = tile("xs_hz_raw", [P, S], U8)
@@ -98,50 +128,45 @@ def tile_picked_hjoinecndotegp_none_po_kernel(
         n3_t = load_list("n3_t", n3)
         n4_t = load_list("n4_t", n4)
         n5_t = load_list("n5_t", n5)
+        tau_t = load_per_row(nc.sync, "tau_t", tau)
 
-        w1 = deal(nc.scalar.copy, "w1", w1_raw, U32)
+        w1 = deal_first_tile_ahead(nc.scalar.copy, "w1", w1_raw, U32)
         w2 = deal(nc.scalar.copy, "w2", w2_raw, U32)
-        w1_s = tile("w1_s", [P, C], U8)
-        by_tile = w1_plane[:].rearrange("p (m t) -> p m t", t=R)
-        nc.vector.tensor_copy(w1_s[:, :P], by_tile[:, :, 0])
-        nc.vector.tensor_copy(w1_s[:, P:].rearrange("p (t m) -> p m t", t=R - 1), by_tile[:, :, 1:])
-        w34_raw = tile("w34_raw", [P, 2 * C], U32, "w1_raw")
-        w3_raw, w4_raw = w34_raw[:, :C], w34_raw[:, C:]
-        for dst, src in ((w3_raw, w3_words), (w4_raw, w4_words)):
-            nc.sync.dma_start(dst.bitcast(I32), src[0].rearrange("p n t -> p (n t)").bitcast(I32))
-        w34_plane = w1_plane
-        load_scale_rows(nc.sync, w34_plane, 0, w3_scales)
-        load_scale_rows(nc.sync, w34_plane, 4, w4_scales)
+        w1_s = deal_first_tile_ahead(nc.vector.tensor_copy, "w1_s", w1_plane, U8)
+
+        w3_first, w4_first = 0, 4
+        w34_raw = tile("w34_raw", [P, 2 * C], U32, after="w1_raw")
+        nc.sync.dma_start(w34_raw[:, :C].bitcast(I32), as_words(w3_words))
+        nc.sync.dma_start(w34_raw[:, C:].bitcast(I32), as_words(w4_words))
+        load_scale_rows(w1_plane, w3_first, w3_scales)
+        load_scale_rows(w1_plane, w4_first, w4_scales)
 
         x_offs = tile("x_offs", [P, S], U32)
         x_hz = tile("x_hz", [P, S], U32)
         nc.vector.tensor_copy(x_offs[:], x_table[:].indirect(offs_t[:]))
         nc.vector.tensor_copy(x_hz[:], x_table[:].indirect(hz_t[:]))
 
-        def mm(out, w, w_s, first, t, rhs, rhs_s, start, stop):
-            cols = slice(P * t, P * (t + 1))
-            nc.tensor.matmul_mx(out=out, lhsT=w[:, cols].bitcast(FP8X4), lhsT_scale=w_s[first:P, cols],
-                                rhs=rhs.bitcast(FP8X4), rhs_scale=rhs_s, start=start, stop=stop)
-
         y_ps = [psum.tile([P, S], F32, name=f"y_ps{t}", tag=f"bank{t}") for t in range(R)]
         d_ps = [psum.tile([P, S], F32, name=f"d_ps{t}", tag=f"bank{R + t}") for t in range(R)]
         for t in range(R):
-            mm(y_ps[t][:], w1, w1_s, 0, t, x_offs[:], xs_offs[:], True, True)
+            product(y_ps[t][:], w1, w1_s, 0, t, x_offs[:], xs_offs[:], True, True)
 
         y_sum = tile("y_sum", [P, R], F32)
         sg_bias = tile("sg_bias", [P, R], F32)
         sg = tile("sg", [P, R, S], F32)
         for t in range(R):
-            nc.vector.tensor_scalar(yh_win[t][:, :S], y_ps[t][:], 1.0, None, ALU.mult, ALU.add, accum_out=y_sum[:, t : t + 1])
-            nc.gpsimd.tensor_scalar(sg_bias[:, t : t + 1], y_sum[:, t : t + 1], -1.0 / S, sl_t[:, t : t + 1], ALU.mult, ALU.mult)
-            nc.scalar.activation(sg[:, t, :], yh_win[t][:].indirect(n1_t[:]), ACT.Sigmoid,
-                                 bias=sg_bias[:, t : t + 1], scale=sl_t[:, t : t + 1])
-        w2_s = deal(nc.vector.tensor_copy, "w2_s", w2_plane, U8, "w1_s")
+            row = slice(t, t + 1)
+            nc.vector.tensor_scalar(yh_win[t][:, :S], y_ps[t][:], 1.0, None, ALU.mult, ALU.add, accum_out=y_sum[:, row])
+            nc.gpsimd.tensor_scalar(sg_bias[:, row], y_sum[:, row], -1.0 / S, sl_t[:, row], ALU.mult, ALU.mult)
+            nc.scalar.activation(sg[:, t, :], yh_win[t][:].indirect(n1_t[:]), ACT.Sigmoid, bias=sg_bias[:, row], scale=sl_t[:, row])
+
+        w2_s = deal_first_tile_ahead(nc.vector.tensor_copy, "w2_s", w2_plane, U8, after="w1_s")
         for t in range(R):
-            mm(d_ps[t][:], w2, w2_s, 0, t, x_hz[:], xs_hz[:], True, True)
+            product(d_ps[t][:], w2, w2_s, 0, t, x_hz[:], xs_hz[:], True, True)
         for t in range(R):
             nc.vector.tensor_copy(d_win[t][:, :S], d_ps[t][:])
 
+        halves = [slice(HALF * half, HALF * (half + 1)) for half in range(2)]
         d2 = tile("d2", [P, R, S], F32)
         d3 = tile("d3", [P, R, S], F32)
         d4 = tile("d4", [P, R, S], F32)
@@ -149,97 +174,99 @@ def tile_picked_hjoinecndotegp_none_po_kernel(
             nc.scalar.activation(d2[:, t, :], d_win[t][:].indirect(n2_t[:]), ACT.Copy, scale=0.75)
         for t in range(R):
             nc.scalar.activation(d3[:, t, :], d_win[t][:].indirect(n3_t[:]), ACT.Copy)
-        for half in range(2):
-            cols = slice(HALF * half, HALF * (half + 1))
+        for cols in halves:
+            offsets = n4_t[:, cols.start // LIST_ROWS : cols.stop // LIST_ROWS]
             for t in range(R):
-                nc.scalar.activation(d4[:, t, cols], d_win[t][:].indirect(n4_t[:, 8 * half : 8 * half + 8]), ACT.Copy, scale=0.75)
+                nc.scalar.activation(d4[:, t, cols], d_win[t][:].indirect(offsets), ACT.Copy, scale=0.75)
 
         neg_mu = tile("neg_mu", [P, R], F32)
-        yc = tile("yc", [P, R, S], F32)
+        y_centred = tile("y_centred", [P, R, S], F32)
         nc.gpsimd.tensor_scalar(neg_mu[:], y_sum[:], -1.0 / S, 0.0, ALU.mult, ALU.add)
         for t in range(R):
-            nc.gpsimd.tensor_scalar(yc[:, t, :], yh_win[t][:, :S], neg_mu[:, t : t + 1], gn_t[:, t : t + 1], ALU.add, ALU.mult)
+            nc.gpsimd.tensor_scalar(y_centred[:, t, :], yh_win[t][:, :S], neg_mu[:, t : t + 1], gn_t[:, t : t + 1], ALU.add, ALU.mult)
 
-        def woven(bf):
-            return bf.rearrange("p (c i t) -> p c t i", i=4, t=R)
-
-        def planar(f):
-            return f.rearrange("p t (c i) -> p c t i", i=4)
-
-        z_bf = tile("z_bf", [P, R * S], BF16, "w2")
+        z_bf = tile("z_bf", [P, R * S], BF16, after="w2")
         z_words = tile("z_words", [P, S], U32)
         z_s = tile("z_s", [P, S], U8)
-        nc.vector.tensor_tensor(woven(z_bf[:]), planar(yc[:]), planar(sg[:]), ALU.mult)
-        pa = tile("pa", [P, R, S], F32)
-        nc.vector.scalar_tensor_tensor(pa[:, 0, :], d_win[0][:, :S], gm_t[:, 0:1], d2[:, 0, :], ALU.mult, ALU.mult)
+        term_a = tile("term_a", [P, R, S], F32)
+
+        def first_term(t):
+            nc.vector.scalar_tensor_tensor(term_a[:, t, :], d_win[t][:, :S], gm_t[:, t : t + 1], d2[:, t, :], ALU.mult, ALU.mult)
+
+        nc.vector.tensor_tensor(woven(z_bf[:]), planar(y_centred[:]), planar(sg[:]), ALU.mult)
+        first_term(0)
         nc.vector.quantize_mx(out=z_words[:].bitcast(FP8X4), scales=z_s[:], in_=z_bf[:])
         for t in range(1, R):
-            nc.vector.scalar_tensor_tensor(pa[:, t, :], d_win[t][:, :S], gm_t[:, t : t + 1], d2[:, t, :], ALU.mult, ALU.mult)
+            first_term(t)
 
-        w34 = tile("w34", [P, 2 * C], U32, "w1_s")
+        w34 = tile("w34", [P, 2 * C], U32, after="w1_s")
         nc.vector.tensor_copy(w34[:].rearrange("p (w t m) -> p w m t", w=2, t=R), w34_raw[:].rearrange("p (w m t) -> p w m t", w=2, t=R))
         w3, w4 = w34[:, :C], w34[:, C:]
-        w34_s = deal(nc.vector.tensor_copy, "w34_s", w34_plane, U8, "w2")
+        w34_s = deal(nc.vector.tensor_copy, "w34_s", w1_plane, U8, after="w2")
 
         h_ps = [psum.tile([P, S], F32, name=f"h_ps{t}", tag=f"bank{t}") for t in range(R)]
         for t in range(R):
-            mm(h_ps[t][:], w3, w34_s, 0, t, z_words[:], z_s[:], True, False)
+            product(h_ps[t][:], w3, w34_s, w3_first, t, z_words[:], z_s[:], True, False)
 
-        for half in range(2):
-            cols = slice(HALF * half, HALF * (half + 1))
+        for half, cols in enumerate(halves):
             z2_bf = tile(f"z2_bf{half}", [P, R * HALF], BF16)
-            pb = tile(f"pb{half}", [P, R, HALF], F32, "z2_bf0" if half else "w1_plane")
+            term_b = tile(f"term_b{half}", [P, R, HALF], F32, after="w1_plane")
             z2_words = tile(f"z2_words{half}", [P, HALF], U32)
             z2_s = tile(f"z2_s{half}", [P, HALF], U8)
             for t in range(R):
-                nc.vector.scalar_tensor_tensor(pb[:, t, :], d3[:, t, cols], gm_t[:, t : t + 1], d4[:, t, cols], ALU.mult, ALU.mult)
-            nc.vector.tensor_tensor(woven(z2_bf[:]), planar(pa[:, :, cols]), planar(pb[:]), ALU.add)
+                nc.vector.scalar_tensor_tensor(term_b[:, t, :], d3[:, t, cols], gm_t[:, t : t + 1], d4[:, t, cols], ALU.mult, ALU.mult)
+            nc.vector.tensor_tensor(woven(z2_bf[:]), planar(term_a[:, :, cols]), planar(term_b[:]), ALU.add)
             nc.vector.quantize_mx(out=z2_words[:].bitcast(FP8X4), scales=z2_s[:], in_=z2_bf[:])
             for t in range(R):
-                mm(h_ps[t][:, cols], w4, w34_s, 4, t, z2_words[:], z2_s[:], False, half == 1)
+                product(h_ps[t][:, cols], w4, w34_s, w4_first, t, z2_words[:], z2_s[:], False, half == 1)
 
         top = tile("top", [P, R], F32)
         ea_bias = tile("ea_bias", [P, R], F32)
         for t in range(R):
-            nc.vector.tensor_scalar(yh_win[t][:, :S], h_ps[t][:], 1.0, None, ALU.mult, ALU.max, accum_out=top[:, t : t + 1])
-            nc.gpsimd.tensor_scalar(ea_bias[:, t : t + 1], top[:, t : t + 1], -1.0, tau_t[:, t : t + 1], ALU.mult, ALU.mult)
+            row = slice(t, t + 1)
+            nc.vector.tensor_scalar(yh_win[t][:, :S], h_ps[t][:], 1.0, None, ALU.mult, ALU.max, accum_out=top[:, row])
+            nc.gpsimd.tensor_scalar(ea_bias[:, row], top[:, row], -1.0, tau_t[:, row], ALU.mult, ALU.mult)
 
         o_words = tile("o_words", [P, S], U32)
         o_s = tile("o_s", [P, S], U8)
         out_rows = out_0.rearrange("(p t) j -> p t j", t=R)
         o_f = [tile(f"o_f{half}", [P, R, HALF], F32) for half in range(2)]
-        ea = [tile(f"ea{half}", [P, R, HALF * 4], F32) for half in range(2)]
+        ea = [tile(f"ea{half}", [P, R, HALF, MEMBERS], F32) for half in range(2)]
         mx = [tile(f"mx{half}", [P, R, HALF], F32) for half in range(2)]
         mn = [tile(f"mn{half}", [P, R, HALF], F32) for half in range(2)]
-        gap = [tile(f"gap{half}", [P, R, HALF], F32) for half in range(2)]
+        spread = [tile(f"spread{half}", [P, R, HALF], F32) for half in range(2)]
         h3 = tile("h3", [P, R, S], F32)
         o_bf = tile("o_bf", [P, R * S], BF16)
         for t in range(R):
             nc.gpsimd.tensor_scalar(h3[:, t, :], yh_win[t][:, :S], 3.0, 0.0, ALU.mult, ALU.add)
 
-        for half in range(2):
-            for t in range(R):
-                for piece in range(2):
-                    c0 = 32 * half + 16 * piece
-                    nc.scalar.activation(ea[half][:, t, S * piece : S * (piece + 1)], yh_win[t][:].indirect(n5_t[:, c0 : c0 + 16]), ACT.Exp,
-                                         bias=ea_bias[:, t : t + 1], scale=tau_t[:, t : t + 1])
+        def is_last(half, t):
+            return half == 1 and t == R - 1
 
-        for half in range(2):
-            cols = slice(HALF * half, HALF * (half + 1))
+        def pieces(half, t):
+            return [slice(0, HALF // 2), slice(HALF // 2, HALF)] if is_last(half, t) else [slice(0, HALF)]
+
+        for half, cols in enumerate(halves):
             for t in range(R):
-                last = half == 1 and t == R - 1
-                members = ea[half][:, t, :].rearrange("p (j m) -> p j m", m=4)
-                for js in (slice(0, 64), slice(64, HALF)) if last else (slice(0, HALF),):
-                    nc.vector.tensor_reduce(mx[half][:, t, js], members[:, js, :], mybir.AxisListType.X, ALU.max)
-                    nc.vector.tensor_reduce(mn[half][:, t, js], members[:, js, :], mybir.AxisListType.X, ALU.min)
-                engine = nc.vector if last else nc.gpsimd
-                engine.tensor_tensor(gap[half][:, t, :], mx[half][:, t, :], mn[half][:, t, :], ALU.subtract)
-                engine.tensor_tensor(o_f[half][:, t, :], gap[half][:, t, :], h3[:, t, cols], ALU.mult)
+                for js in pieces(half, t):
+                    start, stop = (MEMBERS * (cols.start + j) // LIST_ROWS for j in (js.start, js.stop))
+                    nc.scalar.activation(ea[half][:, t, js, :].rearrange("p j m -> p (j m)"), yh_win[t][:].indirect(n5_t[:, start:stop]),
+                                         ACT.Exp, bias=ea_bias[:, t : t + 1], scale=tau_t[:, t : t + 1])
+
+        for half, cols in enumerate(halves):
+            for t in range(R):
+                for js in pieces(half, t):
+                    nc.vector.tensor_reduce(mx[half][:, t, js], ea[half][:, t, js, :], AXIS_X, ALU.max)
+                    nc.vector.tensor_reduce(mn[half][:, t, js], ea[half][:, t, js, :], AXIS_X, ALU.min)
+                engine = nc.vector if is_last(half, t) else nc.gpsimd
+                engine.tensor_tensor(spread[half][:, t, :], mx[half][:, t, :], mn[half][:, t, :], ALU.subtract)
+                engine.tensor_tensor(o_f[half][:, t, :], spread[half][:, t, :], h3[:, t, cols], ALU.mult)
             nc.sync.dma_start(out_rows[:, :, cols], o_f[half][:])
-            copy = nc.vector.tensor_copy if half else nc.scalar.copy
-            copy(woven(o_bf[:, R * HALF * half : R * HALF * (half + 1)]), planar(o_f[half][:]))
+            round_and_weave = nc.vector.tensor_copy if half else nc.scalar.copy
+            round_and_weave(woven(o_bf[:, R * cols.start : R * cols.stop]), planar(o_f[half][:]))
+
         nc.vector.quantize_mx(out=o_words[:].bitcast(FP8X4), scales=o_s[:], in_=o_bf[:])
-        nc.sync.dma_start(out_1[0].rearrange("p n t -> p (n t)").bitcast(I32), o_words[:].bitcast(I32))
-        for q in range(4):
+        nc.sync.dma_start(as_words(out_1), o_words[:].bitcast(I32))
+        for q in range(QUADRANTS):
             queue = nc.scalar if q else nc.sync
             queue.dma_start(out_2[0, 4 * q : 4 * q + 4, :].bitcast(I32), o_s[32 * q : 32 * q + 4, :].bitcast(I32))

from contextlib import ExitStack

import concourse.mybir as mybir

F32 = mybir.dt.float32
BF16 = mybir.dt.bfloat16
I32 = mybir.dt.int32
U32 = mybir.dt.uint32
U16 = mybir.dt.uint16
U8 = mybir.dt.uint8
FP8X4 = mybir.dt.float8_e4m3fn_x4
ALU = mybir.AluOpType
ACT = mybir.ActivationFunctionType
AXIS_X = mybir.AxisListType.X

P = 128
QUADRANTS = 4
T = 2048
S = 256
C = 512
R = 4
HALF = S // 2
MEMBERS = 4
LIST_ROWS = 16
D_WIN = 2 * S
YH_WIN = 4 * S
FLOPS = 4 * 2 * 512 * 512 * 256


def tile_picked_hjoinecndotegp_none_po_kernel(
    tc, x_words, x_scales, w1_words, w1_scales, w2_words, w2_scales, sl, gn, gm,
    w3_words, w3_scales, w4_words, w4_scales, tau, offs, hz, n1, n2, n3, n4, n5,
    out_0, out_1, out_2,
):
    nc = tc.nc
    with ExitStack() as ctx:
        keep = ctx.enter_context(tc.tile_pool(name="keep", bufs=1))
        psum = ctx.enter_context(tc.psum_pool(name="psum", bufs=1))

        def tile(name, shape, dtype, after=None):
            return keep.tile(shape, dtype, name=name, tag=after or name, align_bytes=64)

        def as_words(planes):
            return planes[0].rearrange("p n t -> p (n t)").bitcast(I32)

        def load_list(name, src):
            offsets = keep.tile([P, src.shape[1]], U16, name=name)
            nc.sync.dma_start(offsets[:], src)
            return offsets

        def load_words(name, src, width):
            words = tile(name, [P, width], U32)
            nc.sync.dma_start(words[:].bitcast(I32), as_words(src))
            return words

        def load_scale_rows(plane, first, src):
            for q in range(QUADRANTS):
                rows = plane[32 * q + first : 32 * q + first + 4, :]
                nc.sync.dma_start(rows.bitcast(I32), src[0, 4 * q : 4 * q + 4, :].bitcast(I32))

        def load_per_row(queue, name, src):
            values = tile(name, [P, R], F32)
            queue.dma_start(values[:], src.rearrange("(p t) o -> p (t o)", t=R))
            return values

        def deal(copy, name, src, dtype, after=None):
            dealt = tile(name, [P, C], dtype, after)
            copy(dealt[:].rearrange("p (t m) -> p m t", t=R), src[:].rearrange("p (m t) -> p m t", t=R))
            return dealt

        def deal_first_tile_ahead(copy, name, src, dtype, after=None):
            dealt = tile(name, [P, C], dtype, after)
            by_tile = src[:].rearrange("p (m t) -> p m t", t=R)
            copy(dealt[:, :P], by_tile[:, :, 0])
            copy(dealt[:, P:].rearrange("p (t m) -> p m t", t=R - 1), by_tile[:, :, 1:])
            return dealt

        def product(out, w, w_s, first, t, rhs, rhs_s, start, stop):
            cols = slice(P * t, P * (t + 1))
            nc.tensor.matmul_mx(out=out, lhsT=w[:, cols].bitcast(FP8X4), lhsT_scale=w_s[first:P, cols],
                                rhs=rhs.bitcast(FP8X4), rhs_scale=rhs_s, start=start, stop=stop)

        def woven(bf):
            return bf.rearrange("p (c i t) -> p c t i", i=4, t=R)

        def planar(values):
            return values.rearrange("p t (c i) -> p c t i", i=4)

        x_plane = tile("x_plane", [P, T], U8)
        w1_plane = tile("w1_plane", [P, C], U8)
        w2_plane = tile("w2_plane", [P, C], U8)
        nc.vector.memset(w1_plane[:].bitcast(I32), 0)
        nc.vector.memset(w2_plane[:].bitcast(I32), 0)

        offs_t = load_list("offs_t", offs)
        for q in range(QUADRANTS):
            rows = x_scales[0, 4 * q : 4 * q + 4, :].bitcast(I32)
            nc.sync.dma_start(x_plane[32 * q : 32 * q + 32, :].bitcast(I32), rows.partition_broadcast(8))
        hz_t = load_list("hz_t", hz)
        x_table = load_words("x_table", x_words, T)
        n1_t = load_list("n1_t", n1)
        load_scale_rows(w1_plane, 0, w1_scales)
        w1_raw = load_words("w1_raw", w1_words, C)
        w2_raw = load_words("w2_raw", w2_words, C)
        sl_t = load_per_row(nc.gpsimd, "sl_t", sl)
        load_scale_rows(w2_plane, 0, w2_scales)
        gn_t = load_per_row(nc.gpsimd, "gn_t", gn)
        gm_t = load_per_row(nc.gpsimd, "gm_t", gm)

        yh_win = [tile(f"yh_win{t}", [P, YH_WIN], F32) for t in range(R)]
        d_win = [tile(f"d_win{t}", [P, D_WIN], F32) for t in range(R)]
        for win in yh_win + d_win:
            nc.vector.memset(win[:, S : 2 * S], 0.0)
        for win in yh_win:
            zeros = win[:, S : 2 * S].unsqueeze(1).to_broadcast([P, 2, S])
            nc.scalar.copy(win[:, 2 * S :].rearrange("p (a s) -> p a s", a=2), zeros)

        xs_offs = tile("xs_offs", [P, S], U8)
        xs_hz_raw = tile("xs_hz_raw", [P, S], U8)
        xs_hz = tile("xs_hz", [P, S], U8)
        nc.vector.tensor_copy(xs_hz_raw[:], x_plane[:].indirect(hz_t[:]))
        nc.vector.tensor_copy(xs_hz[:].bitcast(I32), xs_hz_raw[:].bitcast(I32))
        for r in (2, 3):
            nc.sync.dma_start(xs_hz[r:P:32, :].bitcast(I32), xs_hz_raw[16 + r : P : 32, :].bitcast(I32))
        nc.vector.tensor_copy(xs_offs[:], x_plane[:].indirect(offs_t[:]))

        n2_t = load_list("n2_t", n2)
        n3_t = load_list("n3_t", n3)
        n4_t = load_list("n4_t", n4)
        n5_t = load_list("n5_t", n5)
        tau_t = load_per_row(nc.sync, "tau_t", tau)

        w1 = deal_first_tile_ahead(nc.scalar.copy, "w1", w1_raw, U32)
        w2 = deal(nc.scalar.copy, "w2", w2_raw, U32)
        w1_s = deal_first_tile_ahead(nc.vector.tensor_copy, "w1_s", w1_plane, U8)

        w3_first, w4_first = 0, 4
        w34_raw = tile("w34_raw", [P, 2 * C], U32, after="w1_raw")
        nc.sync.dma_start(w34_raw[:, :C].bitcast(I32), as_words(w3_words))
        nc.sync.dma_start(w34_raw[:, C:].bitcast(I32), as_words(w4_words))
        load_scale_rows(w1_plane, w3_first, w3_scales)
        load_scale_rows(w1_plane, w4_first, w4_scales)

        x_offs = tile("x_offs", [P, S], U32)
        x_hz = tile("x_hz", [P, S], U32)
        nc.vector.tensor_copy(x_offs[:], x_table[:].indirect(offs_t[:]))
        nc.vector.tensor_copy(x_hz[:], x_table[:].indirect(hz_t[:]))

        y_ps = [psum.tile([P, S], F32, name=f"y_ps{t}", tag=f"bank{t}") for t in range(R)]
        d_ps = [psum.tile([P, S], F32, name=f"d_ps{t}", tag=f"bank{R + t}") for t in range(R)]
        for t in range(R):
            product(y_ps[t][:], w1, w1_s, 0, t, x_offs[:], xs_offs[:], True, True)

        y_sum = tile("y_sum", [P, R], F32)
        sg_bias = tile("sg_bias", [P, R], F32)
        sg = tile("sg", [P, R, S], F32)
        for t in range(R):
            row = slice(t, t + 1)
            nc.vector.tensor_scalar(yh_win[t][:, :S], y_ps[t][:], 1.0, None, ALU.mult, ALU.add, accum_out=y_sum[:, row])
            nc.gpsimd.tensor_scalar(sg_bias[:, row], y_sum[:, row], -1.0 / S, sl_t[:, row], ALU.mult, ALU.mult)
            nc.scalar.activation(sg[:, t, :], yh_win[t][:].indirect(n1_t[:]), ACT.Sigmoid, bias=sg_bias[:, row], scale=sl_t[:, row])

        w2_s = deal_first_tile_ahead(nc.vector.tensor_copy, "w2_s", w2_plane, U8, after="w1_s")
        for t in range(R):
            product(d_ps[t][:], w2, w2_s, 0, t, x_hz[:], xs_hz[:], True, True)
        for t in range(R):
            nc.vector.tensor_copy(d_win[t][:, :S], d_ps[t][:])

        halves = [slice(HALF * half, HALF * (half + 1)) for half in range(2)]
        d2 = tile("d2", [P, R, S], F32)
        d3 = tile("d3", [P, R, S], F32)
        d4 = tile("d4", [P, R, S], F32)
        for t in range(R):
            nc.scalar.activation(d2[:, t, :], d_win[t][:].indirect(n2_t[:]), ACT.Copy, scale=0.75)
        for t in range(R):
            nc.scalar.activation(d3[:, t, :], d_win[t][:].indirect(n3_t[:]), ACT.Copy)
        for cols in halves:
            offsets = n4_t[:, cols.start // LIST_ROWS : cols.stop // LIST_ROWS]
            for t in range(R):
                nc.scalar.activation(d4[:, t, cols], d_win[t][:].indirect(offsets), ACT.Copy, scale=0.75)

        neg_mu = tile("neg_mu", [P, R], F32)
        y_centred = tile("y_centred", [P, R, S], F32)
        nc.gpsimd.tensor_scalar(neg_mu[:], y_sum[:], -1.0 / S, 0.0, ALU.mult, ALU.add)
        for t in range(R):
            nc.gpsimd.tensor_scalar(y_centred[:, t, :], yh_win[t][:, :S], neg_mu[:, t : t + 1], gn_t[:, t : t + 1], ALU.add, ALU.mult)

        z_bf = tile("z_bf", [P, R * S], BF16, after="w2")
        z_words = tile("z_words", [P, S], U32)
        z_s = tile("z_s", [P, S], U8)
        term_a = tile("term_a", [P, R, S], F32)

        def first_term(t):
            nc.vector.scalar_tensor_tensor(term_a[:, t, :], d_win[t][:, :S], gm_t[:, t : t + 1], d2[:, t, :], ALU.mult, ALU.mult)

        nc.vector.tensor_tensor(woven(z_bf[:]), planar(y_centred[:]), planar(sg[:]), ALU.mult)
        first_term(0)
        nc.vector.quantize_mx(out=z_words[:].bitcast(FP8X4), scales=z_s[:], in_=z_bf[:])
        for t in range(1, R):
            first_term(t)

        w34 = tile("w34", [P, 2 * C], U32, after="w1_s")
        nc.vector.tensor_copy(w34[:].rearrange("p (w t m) -> p w m t", w=2, t=R), w34_raw[:].rearrange("p (w m t) -> p w m t", w=2, t=R))
        w3, w4 = w34[:, :C], w34[:, C:]
        w34_s = deal(nc.vector.tensor_copy, "w34_s", w1_plane, U8, after="w2")

        h_ps = [psum.tile([P, S], F32, name=f"h_ps{t}", tag=f"bank{t}") for t in range(R)]
        for t in range(R):
            product(h_ps[t][:], w3, w34_s, w3_first, t, z_words[:], z_s[:], True, False)

        for half, cols in enumerate(halves):
            z2_bf = tile(f"z2_bf{half}", [P, R * HALF], BF16)
            term_b = tile(f"term_b{half}", [P, R, HALF], F32, after="w1_plane")
            z2_words = tile(f"z2_words{half}", [P, HALF], U32)
            z2_s = tile(f"z2_s{half}", [P, HALF], U8)
            for t in range(R):
                nc.vector.scalar_tensor_tensor(term_b[:, t, :], d3[:, t, cols], gm_t[:, t : t + 1], d4[:, t, cols], ALU.mult, ALU.mult)
            nc.vector.tensor_tensor(woven(z2_bf[:]), planar(term_a[:, :, cols]), planar(term_b[:]), ALU.add)
            nc.vector.quantize_mx(out=z2_words[:].bitcast(FP8X4), scales=z2_s[:], in_=z2_bf[:])
            for t in range(R):
                product(h_ps[t][:, cols], w4, w34_s, w4_first, t, z2_words[:], z2_s[:], False, half == 1)

        top = tile("top", [P, R], F32)
        ea_bias = tile("ea_bias", [P, R], F32)
        for t in range(R):
            row = slice(t, t + 1)
            nc.vector.tensor_scalar(yh_win[t][:, :S], h_ps[t][:], 1.0, None, ALU.mult, ALU.max, accum_out=top[:, row])
            nc.gpsimd.tensor_scalar(ea_bias[:, row], top[:, row], -1.0, tau_t[:, row], ALU.mult, ALU.mult)

        o_words = tile("o_words", [P, S], U32)
        o_s = tile("o_s", [P, S], U8)
        out_rows = out_0.rearrange("(p t) j -> p t j", t=R)
        o_f = [tile(f"o_f{half}", [P, R, HALF], F32) for half in range(2)]
        ea = [tile(f"ea{half}", [P, R, HALF, MEMBERS], F32) for half in range(2)]
        mx = [tile(f"mx{half}", [P, R, HALF], F32) for half in range(2)]
        mn = [tile(f"mn{half}", [P, R, HALF], F32) for half in range(2)]
        spread = [tile(f"spread{half}", [P, R, HALF], F32) for half in range(2)]
        h3 = tile("h3", [P, R, S], F32)
        o_bf = tile("o_bf", [P, R * S], BF16)
        for t in range(R):
            nc.gpsimd.tensor_scalar(h3[:, t, :], yh_win[t][:, :S], 3.0, 0.0, ALU.mult, ALU.add)

        def is_last(half, t):
            return half == 1 and t == R - 1

        def pieces(half, t):
            return [slice(0, HALF // 2), slice(HALF // 2, HALF)] if is_last(half, t) else [slice(0, HALF)]

        for half, cols in enumerate(halves):
            for t in range(R):
                for js in pieces(half, t):
                    start, stop = (MEMBERS * (cols.start + j) // LIST_ROWS for j in (js.start, js.stop))
                    nc.scalar.activation(ea[half][:, t, js, :].rearrange("p j m -> p (j m)"), yh_win[t][:].indirect(n5_t[:, start:stop]),
                                         ACT.Exp, bias=ea_bias[:, t : t + 1], scale=tau_t[:, t : t + 1])

        for half, cols in enumerate(halves):
            for t in range(R):
                for js in pieces(half, t):
                    nc.vector.tensor_reduce(mx[half][:, t, js], ea[half][:, t, js, :], AXIS_X, ALU.max)
                    nc.vector.tensor_reduce(mn[half][:, t, js], ea[half][:, t, js, :], AXIS_X, ALU.min)
                engine = nc.vector if is_last(half, t) else nc.gpsimd
                engine.tensor_tensor(spread[half][:, t, :], mx[half][:, t, :], mn[half][:, t, :], ALU.subtract)
                engine.tensor_tensor(o_f[half][:, t, :], spread[half][:, t, :], h3[:, t, cols], ALU.mult)
            nc.sync.dma_start(out_rows[:, :, cols], o_f[half][:])
            round_and_weave = nc.vector.tensor_copy if half else nc.scalar.copy
            round_and_weave(woven(o_bf[:, R * cols.start : R * cols.stop]), planar(o_f[half][:]))

        nc.vector.quantize_mx(out=o_words[:].bitcast(FP8X4), scales=o_s[:], in_=o_bf[:])
        nc.sync.dma_start(as_words(out_1), o_words[:].bitcast(I32))
        for q in range(QUADRANTS):
            queue = nc.scalar if q else nc.sync
            queue.dma_start(out_2[0, 4 * q : 4 * q + 4, :].bitcast(I32), o_s[32 * q : 32 * q + 4, :].bitcast(I32))
